import numpy as np, ml_dtypes
CORES = [65,73,81,89,97,105,113,121]
N = 8
F = 128
def setup_inputs(rng):
    return {"a": rng.standard_normal((N, 128, 128), dtype=np.float32).astype(ml_dtypes.bfloat16), "w": rng.standard_normal((N, 128, F), dtype=np.float32).astype(ml_dtypes.bfloat16)}
def setup_inputs_big(rng):
    d = setup_inputs(rng)
    for k in ("a", "w"): d[k] = (d[k].astype(np.float32) * 1024.0).astype(d[k].dtype)
    return d
def setup_inputs_small(rng):
    d = setup_inputs(rng)
    for k in ("a", "w"): d[k] = (d[k].astype(np.float32) * (1 / 1024.0)).astype(d[k].dtype)
    return d
def setup_inputs_apart(rng):
    d = setup_inputs(rng)
    f = (10.0 ** rng.permutation(np.linspace(-1.5, 1.5, N))).astype(np.float32).reshape(N, 1, 1)
    for k in ("a", "w"): d[k] = (d[k].astype(np.float32) * f).astype(d[k].dtype)
    return d
def setup_inputs_neg(rng):
    d = setup_inputs(rng)
    d["a"] = (np.abs(d["a"].astype(np.float32)) * 1048576.0).astype(d["a"].dtype); d["w"] = (-np.abs(d["w"].astype(np.float32))).astype(d["w"].dtype)
    return d
def reference(a, w):
    A, W = a.astype(np.float64), w.astype(np.float64)
    p = np.stack([A[j].T @ W[j] for j in range(N)])
    return {"y": np.maximum.accumulate(p, axis=0).astype(ml_dtypes.bfloat16)}

@@ -1,0 +1,119 @@
+from concourse.bass import DstId, RemoteDMATransfer
+from concourse.mybir import AluOpType
+
+F = 128
+NE_RANK = 8
+NE_HELP = 8
+
+SCRATCH = {
+    "a_sb": ("sbuf", [128, 128], "bfloat16"),
+    "w_sb": ("sbuf", [128, F], "bfloat16"),
+    "p": ("psum", [128, F], "float32"),
+    "p_sb": ("sbuf", [128, F], "bfloat16"),
+    "hin": ("sbuf", [128, 4 * F], "bfloat16"),
+    "land0": ("sbuf", [128, F], "bfloat16"),
+    "land1": ("sbuf", [128, F], "bfloat16"),
+    "t_sb": ("sbuf", [128, F], "bfloat16"),
+    "y_sb": ("sbuf", [128, F], "bfloat16"),
+}
+SEMAPHORES = ["ld", "mm", "cp", "got", "sent", "arr0", "arr1", "v1", "done", "st"]
+
+
+def _plan(cores, topo):
+    n = len(cores)
+    chips = [topo.chip(c) for c in cores]
+    partner = [[m for m in range(n) if topo.mates(chips[q], chips[m])][0] for q in range(n)]
+    cls = [0 if (q == 0 or topo.same_plane(chips[q], chips[0])) else 1 for q in range(n)]
+    every = range(topo.CHIPS * topo.CORES_PER_CHIP)
+    helper = [[h for h in every
+               if topo.chip(h) == chips[q] and h not in cores and topo.die(h) == topo.die(cores[q])
+               and topo.may_write(h, cores[partner[q]])][0] for q in range(n)]
+    sets = [[j for j in range(n) if cls[j] == cls[q] and j <= min(q, partner[q])] for q in range(n)]
+    dests = [[d for d in (partner[q], q) if sets[q] and sets[q] != [d]] for q in range(n)]
+    return partner, cls, helper, sets, dests
+
+
+def _engines(topo, src, dsts, count):
+    m = topo.mask(src, dsts[0])
+    for d in dsts[1:]:
+        m &= topo.mask(src, d)
+    bits = [b for b in range(m.bit_length()) if (m >> b) & 1][:count]
+    return sum(1 << b for b in bits)
+
+
+def _ids(topo, dsts):
+    out = []
+    for d in dsts:
+        rid, pid, _se = topo.addr(d)
+        out.append(DstId(rid=rid, pnc=pid))
+    return out
+
+
+def _helper_program(g, core, T, topo, q, plan):
+    partner, cls, helper, sets, dests = plan
+    if not dests[q]:
+        return
+    srcs = [T.hin[:, s * F:(s + 1) * F] for s in range(len(sets[q]))]
+    to = [T.cores[d] for d in dests[q]]
+    land = T["land%d" % cls[q]]
+    g.wait_ge(T.sem.got, NE_RANK * len(sets[q]))
+    g.remote_dma_fused([RemoteDMATransfer(
+        dst_ids=_ids(topo, to), dma_engine_mask=_engines(topo, core, to, NE_HELP),
+        remote_sem=T.sem["arr%d" % cls[q]], srcs=srcs, dsts=[land[:] for _ in to],
+        alu_op=2 if len(srcs) > 1 else 0)], local_sem=T.sem.sent)
+    g.wait_ge(T.sem.sent, NE_HELP)
+
+
+def rank_program(g, core, T, topo):
+    plan = _plan(T.cores, topo)
+    partner, cls, helper, sets, dests = plan
+    r = T.rank_of(core)
+    if r is None:
+        if core in helper:
+            _helper_program(g, core, T, topo, helper.index(core), plan)
+        return
+
+    g.sync.dma_start(T.a_sb[:], T.a[:]).then_inc(T.sem.ld, 16)
+    g.scalar.dma_start(T.w_sb[:], T.w[:]).then_inc(T.sem.ld, 16)
+    g.tensor.wait_ge(T.sem.ld, 32)
+    g.tensor.matmul(T.p[:], T.a_sb[:], T.w_sb[:], True, True).then_inc(T.sem.mm, 1)
+    g.vector.wait_ge(T.sem.mm, 1)
+
+    takers = [q for q in range(len(T.cores) - 1, -1, -1) if r in sets[q] and dests[q]]
+    incoming = [q for q in (r, partner[r]) if r in dests[q]]
+    own = not (r in dests[r] and r in sets[r])
+    if takers or not incoming:
+        g.vector.tensor_copy(T.p_sb[:], T.p[:]).then_inc(T.sem.cp, 1)
+    if takers:
+        to = [helper[q] for q in takers]
+        g.wait_ge(T.sem.cp, 1)
+        g.remote_dma_fused([RemoteDMATransfer(
+            dst_ids=_ids(topo, to), dma_engine_mask=_engines(topo, core, to, NE_RANK),
+            remote_sem=T.sem.got, srcs=[T.p_sb[:]],
+            dsts=[T.hin[:, sets[q].index(r) * F:(sets[q].index(r) + 1) * F] for q in takers],
+            alu_op=0)], local_sem=T.sem.sent)
+
+    if not incoming:
+        g.sync.wait_ge(T.sem.cp, 1)
+        res = T.p_sb
+    else:
+        res = T.y_sb
+        terms = ([T.p] if own else []) + [T["land%d" % cls[q]] for q in incoming]
+        waits = ([None] if own else []) + [T.sem["arr%d" % cls[q]] for q in incoming]
+        acc = terms[0]
+        if waits[0] is not None:
+            g.vector.wait_ge(waits[0], NE_HELP)
+        for i in range(1, len(terms)):
+            last = i == len(terms) - 1
+            g.vector.wait_ge(waits[i], NE_HELP)
+            if i > 1:
+                g.vector.wait_ge(T.sem.v1, 1)
+            out = T.y_sb if last else T.t_sb
+            g.vector.tensor_tensor(out[:], acc[:], terms[i][:], AluOpType.max).then_inc(
+                T.sem.done if last else T.sem.v1, 1)
+            acc = out
+        g.sync.wait_ge(T.sem.done, 1)
+    g.sync.dma_start(T.y[:], res[:]).then_inc(T.sem.st, 16)
+    g.sync.wait_ge(T.sem.st, 16)
+    if takers:
+        g.wait_ge(T.sem.sent, NE_RANK)

@@ -2,8 +2,7 @@ from concourse.bass import DstId, RemoteDMATransfer
 from concourse.mybir import AluOpType
 
 F = 128
-NE_RANK = 8
-NE_HELP = 8
+NE = 8
 
 SCRATCH = {
     "a_sb": ("sbuf", [128, 128], "bfloat16"),
@@ -11,12 +10,11 @@ SCRATCH = {
     "p": ("psum", [128, F], "float32"),
     "p_sb": ("sbuf", [128, F], "bfloat16"),
     "hin": ("sbuf", [128, 4 * F], "bfloat16"),
-    "land0": ("sbuf", [128, F], "bfloat16"),
-    "land1": ("sbuf", [128, F], "bfloat16"),
-    "t_sb": ("sbuf", [128, F], "bfloat16"),
+    "hc": ("sbuf", [128, F], "bfloat16"),
+    "hf": ("sbuf", [128, F], "bfloat16"),
     "y_sb": ("sbuf", [128, F], "bfloat16"),
 }
-SEMAPHORES = ["ld", "mm", "cp", "got", "sent", "arr0", "arr1", "v1", "done", "st"]
+SEMAPHORES = ["ld", "mm", "cp", "got0", "got1", "got2", "got3", "sent", "hc", "hf", "v", "done", "st"]
 
 
 def _plan(cores, topo):
@@ -24,13 +22,13 @@ def _plan(cores, topo):
     chips = [topo.chip(c) for c in cores]
     partner = [[m for m in range(n) if topo.mates(chips[q], chips[m])][0] for q in range(n)]
     cls = [0 if (q == 0 or topo.same_plane(chips[q], chips[0])) else 1 for q in range(n)]
+    slot = [len([j for j in range(q) if cls[j] == cls[q]]) for q in range(n)]
     every = range(topo.CHIPS * topo.CORES_PER_CHIP)
     helper = [[h for h in every
                if topo.chip(h) == chips[q] and h not in cores and topo.die(h) == topo.die(cores[q])
                and topo.may_write(h, cores[partner[q]])][0] for q in range(n)]
     sets = [[j for j in range(n) if cls[j] == cls[q] and j <= min(q, partner[q])] for q in range(n)]
-    dests = [[d for d in (partner[q], q) if sets[q] and sets[q] != [d]] for q in range(n)]
-    return partner, cls, helper, sets, dests
+    return partner, cls, slot, helper, sets
 
 
 def _engines(topo, src, dsts, count):
@@ -49,24 +47,35 @@ def _ids(topo, dsts):
     return out
 
 
-def _helper_program(g, core, T, topo, q, plan):
-    partner, cls, helper, sets, dests = plan
-    if not dests[q]:
-        return
-    srcs = [T.hin[:, s * F:(s + 1) * F] for s in range(len(sets[q]))]
-    to = [T.cores[d] for d in dests[q]]
-    land = T["land%d" % cls[q]]
-    g.wait_ge(T.sem.got, NE_RANK * len(sets[q]))
+def _send(g, T, topo, core, to, srcs, dsts, sem):
     g.remote_dma_fused([RemoteDMATransfer(
-        dst_ids=_ids(topo, to), dma_engine_mask=_engines(topo, core, to, NE_HELP),
-        remote_sem=T.sem["arr%d" % cls[q]], srcs=srcs, dsts=[land[:] for _ in to],
-        alu_op=2 if len(srcs) > 1 else 0)], local_sem=T.sem.sent)
-    g.wait_ge(T.sem.sent, NE_HELP)
+        dst_ids=_ids(topo, to), dma_engine_mask=_engines(topo, core, to, NE),
+        remote_sem=sem, srcs=srcs, dsts=dsts, alu_op=2 if len(srcs) > 1 else 0)], local_sem=T.sem.sent)
+
+
+def _slot(T, s):
+    return T.hin[:, s * F:(s + 1) * F]
+
+
+def _helper_program(g, core, T, topo, q, plan):
+    partner, cls, slot, helper, sets = plan
+    if not sets[q]:
+        return
+    to = [T.cores[partner[q]]]
+    first, rest = sets[q][-1], sets[q][:-1]
+    g.wait_ge(T.sem["got%d" % slot[first]], NE)
+    _send(g, T, topo, core, to, [_slot(T, slot[first])], [T.hc[:]], T.sem.hc)
+    if rest:
+        for j in reversed(rest):
+            g.wait_ge(T.sem["got%d" % slot[j]], NE)
+        _send(g, T, topo, core, to, [_slot(T, slot[j]) for j in rest], [T.hf[:]], T.sem.hf)
+    g.wait_ge(T.sem.sent, NE * (2 if rest else 1))
 
 
 def rank_program(g, core, T, topo):
     plan = _plan(T.cores, topo)
-    partner, cls, helper, sets, dests = plan
+    partner, cls, slot, helper, sets = plan
+    n = len(T.cores)
     r = T.rank_of(core)
     if r is None:
         if core in helper:
@@ -79,41 +88,44 @@ def rank_program(g, core, T, topo):
     g.tensor.matmul(T.p[:], T.a_sb[:], T.w_sb[:], True, True).then_inc(T.sem.mm, 1)
     g.vector.wait_ge(T.sem.mm, 1)
 
-    takers = [q for q in range(len(T.cores) - 1, -1, -1) if r in sets[q] and dests[q]]
-    incoming = [q for q in (r, partner[r]) if r in dests[q]]
-    own = not (r in dests[r] and r in sets[r])
-    if takers or not incoming:
+    takers = [q for q in range(n - 1, -1, -1) if r in sets[q]]
+    peers = [m for m in range(n - 1, r, -1) if cls[m] == cls[r]]
+    cross = sets[partner[r]]
+    incoming = [(T.sem["got%d" % slot[j]], _slot(T, slot[j])) for j in range(r - 1, -1, -1) if cls[j] == cls[r]]
+    if cross:
+        incoming.append((T.sem.hc, T.hc[:]))
+    if len(cross) > 1:
+        incoming.append((T.sem.hf, T.hf[:]))
+
+    rounded = bool(takers or peers or not incoming)
+    if rounded:
         g.vector.tensor_copy(T.p_sb[:], T.p[:]).then_inc(T.sem.cp, 1)
-    if takers:
-        to = [helper[q] for q in takers]
+    calls = 0
+    if takers or peers:
         g.wait_ge(T.sem.cp, 1)
-        g.remote_dma_fused([RemoteDMATransfer(
-            dst_ids=_ids(topo, to), dma_engine_mask=_engines(topo, core, to, NE_RANK),
-            remote_sem=T.sem.got, srcs=[T.p_sb[:]],
-            dsts=[T.hin[:, sets[q].index(r) * F:(sets[q].index(r) + 1) * F] for q in takers],
-            alu_op=0)], local_sem=T.sem.sent)
+    for group in ([helper[q] for q in takers], [T.cores[m] for m in peers]):
+        if group:
+            _send(g, T, topo, core, group, [T.p_sb[:]], [_slot(T, slot[r]) for _ in group],
+                  T.sem["got%d" % slot[r]])
+            calls += 1
 
     if not incoming:
         g.sync.wait_ge(T.sem.cp, 1)
         res = T.p_sb
     else:
         res = T.y_sb
-        terms = ([T.p] if own else []) + [T["land%d" % cls[q]] for q in incoming]
-        waits = ([None] if own else []) + [T.sem["arr%d" % cls[q]] for q in incoming]
-        acc = terms[0]
-        if waits[0] is not None:
-            g.vector.wait_ge(waits[0], NE_HELP)
-        for i in range(1, len(terms)):
-            last = i == len(terms) - 1
-            g.vector.wait_ge(waits[i], NE_HELP)
-            if i > 1:
-                g.vector.wait_ge(T.sem.v1, 1)
-            out = T.y_sb if last else T.t_sb
-            g.vector.tensor_tensor(out[:], acc[:], terms[i][:], AluOpType.max).then_inc(
-                T.sem.done if last else T.sem.v1, 1)
-            acc = out
+        for i, (sem, buf) in enumerate(incoming):
+            last = i == len(incoming) - 1
+            g.vector.wait_ge(sem, NE)
+            if i:
+                g.vector.wait_ge(T.sem.v, i)
+            elif rounded:
+                g.vector.wait_ge(T.sem.cp, 1)
+            out = T.y_sb if last else T.p
+            g.vector.tensor_tensor(out[:], T.p[:], buf, AluOpType.max).then_inc(
+                T.sem.done if last else T.sem.v, 1)
         g.sync.wait_ge(T.sem.done, 1)
     g.sync.dma_start(T.y[:], res[:]).then_inc(T.sem.st, 16)
     g.sync.wait_ge(T.sem.st, 16)
-    if takers:
-        g.wait_ge(T.sem.sent, NE_RANK)
+    if calls:
+        g.wait_ge(T.sem.sent, NE * calls)

from concourse.bass import DstId, RemoteDMATransfer
from concourse.mybir import AluOpType

F = 128
NE = 8

SCRATCH = {
    "a_sb": ("sbuf", [128, 128], "bfloat16"),
    "w_sb": ("sbuf", [128, F], "bfloat16"),
    "p": ("psum", [128, F], "float32"),
    "p_sb": ("sbuf", [128, F], "bfloat16"),
    "hin": ("sbuf", [128, 4 * F], "bfloat16"),
    "hc": ("sbuf", [128, F], "bfloat16"),
    "hf": ("sbuf", [128, F], "bfloat16"),
    "y_sb": ("sbuf", [128, F], "bfloat16"),
}
SEMAPHORES = ["ld", "mm", "cp", "got0", "got1", "got2", "got3", "sent", "hc", "hf", "v", "done", "st"]


def _plan(cores, topo):
    n = len(cores)
    chips = [topo.chip(c) for c in cores]
    partner = [[m for m in range(n) if topo.mates(chips[q], chips[m])][0] for q in range(n)]
    cls = [0 if (q == 0 or topo.same_plane(chips[q], chips[0])) else 1 for q in range(n)]
    slot = [len([j for j in range(q) if cls[j] == cls[q]]) for q in range(n)]
    every = range(topo.CHIPS * topo.CORES_PER_CHIP)
    helper = [[h for h in every
               if topo.chip(h) == chips[q] and h not in cores and topo.die(h) == topo.die(cores[q])
               and topo.may_write(h, cores[partner[q]])][0] for q in range(n)]
    sets = [[j for j in range(n) if cls[j] == cls[q] and j <= min(q, partner[q])] for q in range(n)]
    return partner, cls, slot, helper, sets


def _engines(topo, src, dsts, count):
    m = topo.mask(src, dsts[0])
    for d in dsts[1:]:
        m &= topo.mask(src, d)
    bits = [b for b in range(m.bit_length()) if (m >> b) & 1][:count]
    return sum(1 << b for b in bits)


def _ids(topo, dsts):
    out = []
    for d in dsts:
        rid, pid, _se = topo.addr(d)
        out.append(DstId(rid=rid, pnc=pid))
    return out


def _send(g, T, topo, core, to, srcs, dsts, sem):
    g.remote_dma_fused([RemoteDMATransfer(
        dst_ids=_ids(topo, to), dma_engine_mask=_engines(topo, core, to, NE),
        remote_sem=sem, srcs=srcs, dsts=dsts, alu_op=2 if len(srcs) > 1 else 0)], local_sem=T.sem.sent)


def _slot(T, s):
    return T.hin[:, s * F:(s + 1) * F]


def _helper_program(g, core, T, topo, q, plan):
    partner, cls, slot, helper, sets = plan
    if not sets[q]:
        return
    to = [T.cores[partner[q]]]
    first, rest = sets[q][-1], sets[q][:-1]
    g.wait_ge(T.sem["got%d" % slot[first]], NE)
    _send(g, T, topo, core, to, [_slot(T, slot[first])], [T.hc[:]], T.sem.hc)
    if rest:
        for j in reversed(rest):
            g.wait_ge(T.sem["got%d" % slot[j]], NE)
        _send(g, T, topo, core, to, [_slot(T, slot[j]) for j in rest], [T.hf[:]], T.sem.hf)
    g.wait_ge(T.sem.sent, NE * (2 if rest else 1))


def rank_program(g, core, T, topo):
    plan = _plan(T.cores, topo)
    partner, cls, slot, helper, sets = plan
    n = len(T.cores)
    r = T.rank_of(core)
    if r is None:
        if core in helper:
            _helper_program(g, core, T, topo, helper.index(core), plan)
        return

    g.sync.dma_start(T.a_sb[:], T.a[:]).then_inc(T.sem.ld, 16)
    g.scalar.dma_start(T.w_sb[:], T.w[:]).then_inc(T.sem.ld, 16)
    g.tensor.wait_ge(T.sem.ld, 32)
    g.tensor.matmul(T.p[:], T.a_sb[:], T.w_sb[:], True, True).then_inc(T.sem.mm, 1)
    g.vector.wait_ge(T.sem.mm, 1)

    takers = [q for q in range(n - 1, -1, -1) if r in sets[q]]
    peers = [m for m in range(n - 1, r, -1) if cls[m] == cls[r]]
    cross = sets[partner[r]]
    incoming = [(T.sem["got%d" % slot[j]], _slot(T, slot[j])) for j in range(r - 1, -1, -1) if cls[j] == cls[r]]
    if cross:
        incoming.append((T.sem.hc, T.hc[:]))
    if len(cross) > 1:
        incoming.append((T.sem.hf, T.hf[:]))

    rounded = bool(takers or peers or not incoming)
    if rounded:
        g.vector.tensor_copy(T.p_sb[:], T.p[:]).then_inc(T.sem.cp, 1)
    calls = 0
    if takers or peers:
        g.wait_ge(T.sem.cp, 1)
    for group in ([helper[q] for q in takers], [T.cores[m] for m in peers]):
        if group:
            _send(g, T, topo, core, group, [T.p_sb[:]], [_slot(T, slot[r]) for _ in group],
                  T.sem["got%d" % slot[r]])
            calls += 1

    if not incoming:
        g.sync.wait_ge(T.sem.cp, 1)
        res = T.p_sb
    else:
        res = T.y_sb
        for i, (sem, buf) in enumerate(incoming):
            last = i == len(incoming) - 1
            g.vector.wait_ge(sem, NE)
            if i:
                g.vector.wait_ge(T.sem.v, i)
            elif rounded:
                g.vector.wait_ge(T.sem.cp, 1)
            out = T.y_sb if last else T.p
            g.vector.tensor_tensor(out[:], T.p[:], buf, AluOpType.max).then_inc(
                T.sem.done if last else T.sem.v, 1)
        g.sync.wait_ge(T.sem.done, 1)
    g.sync.dma_start(T.y[:], res[:]).then_inc(T.sem.st, 16)
    g.sync.wait_ge(T.sem.st, 16)
    if calls:
        g.wait_ge(T.sem.sent, NE * calls)
